import numpy as np
import ml_dtypes


def mxq(x, axis, fmt="e4m3"):
    dtype, down = {"e4m3": (ml_dtypes.float8_e4m3fn, 7), "e5m2": (ml_dtypes.float8_e5m2, 14)}[fmt]
    v = np.moveaxis(np.asarray(x, np.float32).astype(ml_dtypes.bfloat16).astype(np.float64), axis, -1)
    blocks = v.reshape(v.shape[:-1] + (-1, 32))
    amax = np.abs(blocks).max(-1, keepdims=True)
    byte = np.maximum(np.where(amax > 0, np.frexp(amax)[1] - 1 + 127, 0) - down, 1)
    scale = np.exp2(byte - 127.0)
    codes = (blocks / scale).astype(np.float32).astype(dtype).astype(np.float64)
    return np.moveaxis((codes * scale).reshape(v.shape), -1, axis)


WIDE = False


def mx_kscale(k):
    if not WIDE:
        return np.ones(k)
    levels = np.array([10, -10, 5, -5, 0])
    if k % 512:
        return np.exp2(np.random.permutation(np.resize(levels, k // 32))).repeat(32)
    a = np.empty((k // 512, 16))
    for p in range(k // 512):
        a[p, :8] = np.random.permutation(np.resize(levels, 8))
        for g in range(8):
            far = levels[np.abs(levels - a[p, g]) >= 10]
            a[p, g + 8] = far[np.random.randint(len(far))]
    return np.exp2(a.ravel()).repeat(32)


BF16 = ml_dtypes.bfloat16


def bf(x):
    return np.asarray(x, np.float32).astype(BF16)


def f64(x):
    return np.asarray(x).astype(np.float64)


E2M1 = np.array([0.0, 0.5, 1.0, 1.5, 2.0, 3.0, 4.0, 6.0, -0.0, -0.5, -1.0, -1.5, -2.0, -3.0, -4.0, -6.0])


def pack_weight(w, fmt):
    k, n = w.shape
    w = f64(bf(w)).reshape(k // 32, 32, n)
    amax = np.abs(w).max(1)
    if fmt == "e4m3":
        byte = np.frexp(amax)[1] - 1 + 127 - 7
    else:
        mant, ex = np.frexp(amax / 6.0)
        byte = np.where(mant > 0.5, ex, ex - 1) + 127
    byte = np.clip(np.where(amax > 0, byte, 1), 1, 254)
    scaled = (w * np.exp2(127.0 - byte)[:, None, :]).reshape(k, n).astype(np.float32)
    by_word = np.ascontiguousarray(scaled.reshape(k // 512, 128, 4, n).transpose(0, 1, 3, 2))
    if fmt == "e4m3":
        words = by_word.astype(ml_dtypes.float8_e4m3fn).view(np.uint8)
    else:
        c = by_word.astype(ml_dtypes.float4_e2m1fn).view(np.uint8) & 0xF
        words = c[..., 0::2] | (c[..., 1::2] << 4)
    return np.ascontiguousarray(words), np.ascontiguousarray(byte.astype(np.uint8).reshape(k // 512, 16, n))


def unpack_weight(words, scales, fmt):
    g, p, n, _ = words.shape
    if fmt == "e4m3":
        vals = np.ascontiguousarray(words).view(ml_dtypes.float8_e4m3fn).astype(np.float64)
    else:
        nib = np.empty((g, p, n, 4), np.uint8)
        nib[..., 0::2] = words & 0xF
        nib[..., 1::2] = words >> 4
        vals = E2M1[nib]
    vals = vals * np.repeat(np.exp2(scales.astype(np.float64) - 127.0), 8, axis=1)[..., None]
    return vals.transpose(0, 1, 3, 2).reshape(g * 512, n)
def pack4(w):
    words, scales = pack_weight(w, "e2m1")
    return words.reshape(words.shape[0], 128, -1), scales


def unpack4(words, scales):
    return unpack_weight(words.reshape(words.shape[0], 128, -1, 2), scales, "e2m1")


M, FS, FR, D, N = 1024, 1024, 2048, 1024, 1536


def draw0():
    s, u, t = mx_kscale(FS), mx_kscale(FR), mx_kscale(D)
    hs = bf(np.random.standard_normal((M, FS)) * s)
    hr = bf(np.random.standard_normal((M, FR)) * u)
    gate = bf(np.random.uniform(0.4, 1.0, M))
    ws = bf(np.random.standard_normal((FS, D)) / np.sqrt(FS) / s[:, None])
    wr_words, wr_scales = pack4(np.random.standard_normal((FR, D)) / np.sqrt(FR) / u[:, None])
    gain = bf((1 + 0.1 * np.random.standard_normal(D)) * t)
    resid = bf(np.random.standard_normal((M, D)) * t)
    wo_words, wo_scales = pack4(np.random.standard_normal((D, N)) / np.sqrt(D) / t[:, None])
    return {"hs": hs, "hr": hr, "gate": gate, "ws": ws, "wr_words": wr_words, "wr_scales": wr_scales,
            "gain": gain, "resid": resid, "wo_words": wo_words, "wo_scales": wo_scales}


def core(hs, hr, gate, ws, wr_words, wr_scales, gain, resid, wo_words, wo_scales):
    routed = f64(hr) * f64(gate)[:, None]
    hs_q = mxq(f64(hs), 1, "e4m3")
    ws_q = mxq(f64(ws), 0, "e4m3")
    routed_q = mxq(routed, 1, "e4m3")
    wr = unpack4(wr_words, wr_scales)
    pair = (hs_q @ ws_q) + (routed_q @ wr)
    z = pair * f64(gain) + f64(resid)
    wo = unpack4(wo_words, wo_scales)
    return mxq(z, 1, "e4m3") @ wo


def e4m3fn_bytes(y):
    return np.clip(np.asarray(y, np.float64), -448.0, 448.0).astype(np.float32).astype(ml_dtypes.float8_e4m3fn).view(np.uint8)


def e4m3fn_values(b):
    return np.asarray(b, np.uint8).view(ml_dtypes.float8_e4m3fn).astype(np.float64)


def setup_inputs():
    d = draw0()
    x0 = np.asarray(d['ws']).astype(np.float64)
    s = (np.max(np.abs(x0), axis=(1,), keepdims=True) / 448.0).astype(np.float32)
    out = {}
    for k, v in d.items():
        if k == 'ws':
            out['ws_bytes'] = e4m3fn_bytes(x0 / s.astype(np.float64))
            out['ws_scale'] = s
        else:
            out[k] = v
    return out


def reference(hs, hr, gate, ws_bytes, ws_scale, wr_words, wr_scales, gain, resid, wo_words, wo_scales):
    return core(hs, hr, gate, e4m3fn_values(ws_bytes) * ws_scale.astype(np.float64), wr_words, wr_scales, gain, resid, wo_words, wo_scales)

@@ -1,0 +1,444 @@
+from contextlib import ExitStack
+
+import concourse.mybir as mybir
+from concourse.masks import make_identity
+
+TOKENS, SHARED, ROUTED, CHANNELS, FEATURES = 1024, 1024, 2048, 1024, 1536
+
+FLOPS = 2 * TOKENS * CHANNELS * (SHARED + ROUTED) + 2 * TOKENS * CHANNELS * FEATURES
+
+F32 = mybir.dt.float32
+BF16 = mybir.dt.bfloat16
+I32 = mybir.dt.int32
+U32 = mybir.dt.uint32
+U8 = mybir.dt.uint8
+FP8 = mybir.dt.float8_e4m3fn
+FP8X4 = mybir.dt.float8_e4m3fn_x4
+FP4X4 = mybir.dt.float4_e2m1fn_x4
+MULT = mybir.AluOpType.mult
+ADD = mybir.AluOpType.add
+COPY = mybir.ActivationFunctionType.Copy
+
+P = 128
+K_PASS = 512
+BANK = 512
+TILES = TOKENS // P
+R_PASSES = ROUTED // K_PASS
+S_PASSES = SHARED // K_PASS
+HALVES = CHANNELS // BANK
+OUT_BANKS = FEATURES // BANK
+PLAIN = 3
+LAG = 3
+
+
+def tile_expert_pair_project_s3_kernel(
+    tc, hs, hr, gate, ws_bytes, ws_scale, wr_words, wr_scales, gain, resid, wo_words, wo_scales, out
+):
+    nc = tc.nc
+    with ExitStack() as ctx:
+        keep = ctx.enter_context(tc.tile_pool(name="keep", bufs=1))
+        work = ctx.enter_context(tc.tile_pool(name="work", bufs=3))
+        psum = ctx.enter_context(tc.psum_pool(name="psum", bufs=1))
+        ctx.enter_context(tc.manual_schedule())
+
+        hs_rows = hs.rearrange("(p i) k -> p i k", i=TILES)
+        hr_rows = hr.rearrange("(p i) k -> p i k", i=TILES)
+        resid_rows = resid.rearrange("(p i) d -> p i d", i=TILES)
+        out_rows = out.rearrange("(p i) n -> p i n", i=TILES)
+
+        gate_sb = keep.tile([P, TILES], BF16, name="gate_sb")
+        ws_scale_sb = keep.tile([P, S_PASSES, 4], F32, name="ws_scale_sb")
+        wr_sb = keep.tile([P, R_PASSES, 2 * CHANNELS], U8, name="wr_sb", align_bytes=256)
+        wr_planes = keep.tile([P, R_PASSES, CHANNELS // 4], I32, name="wr_planes", align_bytes=256)
+        wo_sb = keep.tile([P, HALVES, 2 * FEATURES], U8, name="wo_sb", align_bytes=256)
+        wo_planes = keep.tile([P, HALVES, FEATURES // 4], I32, name="wo_planes", align_bytes=256)
+        ident = keep.tile([P, P], F32, name="ident")
+        ones = keep.tile([P, P], BF16, name="ones")
+        gain_row = keep.tile([P, CHANNELS], BF16, name="gain_row")
+        gain_sb = keep.tile([P, CHANNELS], F32, name="gain_sb")
+        hr_sb = [keep.tile([P, ROUTED], BF16, name="hr%d" % i) for i in range(TILES)]
+        hs_sb = [keep.tile([P, SHARED], BF16, name="hs%d" % i) for i in range(TILES)]
+        resid_sb = [keep.tile([P, CHANNELS], BF16, name="resid%d" % i) for i in range(TILES)]
+        ws_raw = [keep.tile([P, 4, CHANNELS], U8, name="ws_raw%d" % g) for g in range(S_PASSES)]
+        ws_wide = [keep.tile([P, 4, CHANNELS], BF16, name="ws_wide%d" % g) for g in range(S_PASSES)]
+        ws_codes = [[keep.tile([P, BANK], U32, name="ws_codes%d%d" % (g, h), align_bytes=256) for h in range(HALVES)] for g in range(S_PASSES)]
+        ws_planes = [[keep.tile([P, BANK], U8, name="ws_planes%d%d" % (g, h), align_bytes=256) for h in range(HALVES)] for g in range(S_PASSES)]
+
+        live = {}
+
+        def load_hr(i, b=None):
+            cols = slice(0, ROUTED) if b is None else slice(b * 1024, (b + 1) * 1024)
+            nc.sync.dma_start(out=hr_sb[i][:, cols], in_=hr_rows[:, i, cols])
+
+        def load_hs(i):
+            nc.sync.dma_start(out=hs_sb[i][:], in_=hs_rows[:, i, :])
+
+        def load_resid(i):
+            nc.sync.dma_start(out=resid_sb[i][:], in_=resid_rows[:, i, :])
+
+        def load_wr(g):
+            nc.sync.dma_start(out=wr_sb[:, g : g + 2, :], in_=wr_words[g : g + 2].rearrange("g p n -> p g n"))
+
+        def load_ws(g):
+            nc.sync.dma_start(out=ws_raw[g][:], in_=ws_bytes.rearrange("(g p t) n -> g p t n", p=P, t=4)[g])
+
+        def load_planes(planes, scales):
+            words = scales.bitcast(I32)
+            for r in range(4):
+                nc.sync.dma_start(out=planes[r:P:32, :, :], in_=words[:, r:16:4, :].rearrange("g q n -> q g n"))
+
+        def apply_gate(i, b):
+            gated = work.tile([P, 1024], BF16, name="gated", bufs=6)
+            dst = gated[:]
+            src = hr_sb[i][:, b * 1024 : (b + 1) * 1024]
+            if i >= PLAIN:
+                dst = dst.rearrange("p (u w e) -> p u w e", u=2, e=2)
+                src = src.rearrange("p (w u e) -> p u w e", u=2, e=2)
+            nc.vector.tensor_scalar(out=dst, in0=src, scalar1=gate_sb[:, i : i + 1], scalar2=None, op0=MULT)
+            live["act", i, b] = gated
+
+        def order_hs(i, engine=None):
+            if i < PLAIN:
+                live["act", i, 2] = hs_sb[i]
+                return
+            ordered = work.tile([P, 1024], BF16, name="ordered", bufs=4)
+            dst = ordered[:].bitcast(F32).rearrange("p (u w) -> p u w", u=2)
+            src = hs_sb[i][:].bitcast(F32).rearrange("p (w u) -> p u w", u=2)
+            if engine == "v":
+                nc.vector.tensor_copy(out=dst, in_=src)
+            else:
+                nc.scalar.copy(out=dst, in_=src)
+            live["act", i, 2] = ordered
+
+        def bank_tile(k, shape):
+            return psum.tile(shape, F32, name="bank%d" % k)
+
+        def next_bank():
+            live["bank"] = (live["bank"] + 1) % 8
+            return live["bank"]
+
+        def turn(key, k=None):
+            words = live[key][:].bitcast(F32)
+            bank = bank_tile(next_bank() if k is None else k, [P, 2, 2, P])
+            plain = key[0] == "act" and key[1] < PLAIN
+            for g in range(2):
+                for u in range(2):
+                    if plain:
+                        block = words[:, 2 * P * g + u : 2 * P * (g + 1) : 2]
+                    else:
+                        block = words[:, (2 * u + g) * P : (2 * u + g + 1) * P]
+                    nc.tensor.transpose(bank[:, g, u, :], block, ident[:])
+            live["T", key] = bank
+
+        def collect(key, engine=None):
+            grouped = work.tile([P, 1024], BF16, name="grouped", bufs=6, align_bytes=256)
+            dst = grouped[:].bitcast(F32).rearrange("p (g r u) -> p g r u", g=2, u=2)
+            src = live["T", key][:].rearrange("p g u r -> p g r u")
+            if engine == "v":
+                nc.vector.tensor_copy(out=dst, in_=src)
+            else:
+                nc.scalar.copy(out=dst, in_=src)
+            live["G", key] = grouped
+
+        def quantize(key):
+            codes = work.tile([P, 2 * P], U32, name="codes", bufs=12, align_bytes=256)
+            planes = work.tile([P, 2 * P], U8, name="planes", bufs=12, align_bytes=256)
+            nc.vector.quantize_mx(out=codes[:].bitcast(FP8X4), scales=planes[:], in_=live["G", key][:])
+            live["Q", key] = (codes, planes)
+
+        def widen(g, t, engine=None):
+            dst = ws_wide[g][:, t, :]
+            src = ws_raw[g][:, t, :].bitcast(FP8)
+            scale = ws_scale_sb[:, g, t : t + 1]
+            if engine == "v":
+                nc.vector.tensor_scalar(out=dst, in0=src, scalar1=scale, scalar2=None, op0=MULT)
+            else:
+                nc.scalar.activation(out=dst, in_=src, func=COPY, scale=scale)
+
+        def interleave(g, h, engine=None):
+            packed = work.tile([P, BANK, 4], BF16, name="packed", bufs=4, align_bytes=256)
+            src = ws_wide[g][:, :, h * BANK : (h + 1) * BANK].rearrange("p t n -> p n t")
+            if engine == "s":
+                nc.scalar.copy(out=packed[:], in_=src)
+            else:
+                nc.vector.tensor_copy(out=packed[:], in_=src)
+            live["W", g, h] = packed
+
+        def quantize_ws(g, h):
+            nc.vector.quantize_mx(
+                out=ws_codes[g][h][:].bitcast(FP8X4),
+                scales=ws_planes[g][h][:],
+                in_=live["W", g, h][:].rearrange("p n t -> p (n t)"),
+            )
+
+        def open_half(i, h, k=None):
+            live["pair", i, h] = bank_tile(next_bank() if k is None else k, [P, BANK])
+
+        def lhs(key, g):
+            codes, planes = live["Q", key]
+            cols = slice(g * P, (g + 1) * P)
+            return codes[:, cols].bitcast(FP8X4), planes[:, cols]
+
+        def routed_pass(i, h, g):
+            codes, planes = lhs(("act", i, g // 2), g % 2)
+            nc.tensor.matmul_mx(
+                out=live["pair", i, h][:],
+                lhsT=codes,
+                lhsT_scale=planes,
+                rhs=wr_sb[:, g, 2 * h * BANK : 2 * (h + 1) * BANK].bitcast(FP4X4),
+                rhs_scale=wr_planes[:, g, h * BANK // 4 : (h + 1) * BANK // 4].bitcast(U8),
+                start=(g == 0),
+                stop=False,
+            )
+
+        def shared_pass(i, h, g):
+            codes, planes = lhs(("act", i, 2), g)
+            nc.tensor.matmul_mx(
+                out=live["pair", i, h][:],
+                lhsT=codes,
+                lhsT_scale=planes,
+                rhs=ws_codes[g][h][:].bitcast(FP8X4),
+                rhs_scale=ws_planes[g][h][:],
+                start=False,
+                stop=(g == S_PASSES - 1),
+            )
+
+        def scale_pair(i, h):
+            scaled = work.tile([P, BANK], F32, name="scaled", bufs=8)
+            nc.vector.tensor_tensor(
+                out=scaled[:], in0=live["pair", i, h][:], in1=gain_sb[:, h * BANK : (h + 1) * BANK], op=MULT
+            )
+            live["scaled", i, h] = scaled
+
+        def add_resid(i, h):
+            if h == 0:
+                live["z", i] = work.tile([P, 1024], BF16, name="z", bufs=4)
+            order = "p (w u e) -> p u w e"
+            nc.vector.tensor_tensor(
+                out=live["z", i][:].rearrange("p (u g w e) -> p g u w e", u=2, g=2, e=2)[:, h],
+                in0=live["scaled", i, h][:].rearrange(order, u=2, e=2),
+                in1=resid_sb[i][:, h * BANK : (h + 1) * BANK].rearrange(order, u=2, e=2),
+                op=ADD,
+            )
+
+        def project(i, n):
+            bank = bank_tile(next_bank(), [P, BANK])
+            for g in range(HALVES):
+                codes, planes = lhs(("z", i), g)
+                nc.tensor.matmul_mx(
+                    out=bank[:],
+                    lhsT=codes,
+                    lhsT_scale=planes,
+                    rhs=wo_sb[:, g, 2 * n * BANK : 2 * (n + 1) * BANK].bitcast(FP4X4),
+                    rhs_scale=wo_planes[:, g, n * BANK // 4 : (n + 1) * BANK // 4].bitcast(U8),
+                    start=(g == 0),
+                    stop=(g == HALVES - 1),
+                )
+            live["out", i, n] = bank
+
+        def empty(i, n, engine=None):
+            if n == 0:
+                live["res", i] = work.tile([P, FEATURES], F32, name="result", bufs=3)
+            dst = live["res", i][:, n * BANK : (n + 1) * BANK]
+            if engine == "v":
+                nc.vector.tensor_copy(out=dst, in_=live["out", i, n][:])
+            else:
+                nc.scalar.copy(out=dst, in_=live["out", i, n][:])
+
+        def store(i, n=None):
+            cols = slice(0, FEATURES) if n is None else slice(n * BANK, (n + 1) * BANK)
+            nc.sync.dma_start(out=out_rows[:, i, cols], in_=live["res", i][:, cols])
+
+        warm = keep.tile([P, 2], F32, name="warm")
+        nc.vector.memset(warm[:], 0.0)
+        nc.vector.memset(wr_planes[:], 0)
+        make_identity(nc, ident[:])
+        nc.gpsimd.memset(ones[:], 1.0)
+        nc.gpsimd.memset(gain_row[:].bitcast(I32), 0)
+        nc.vector.memset(wo_planes[:], 0)
+        nc.scalar.activation(out=warm[:, 1:2], in_=warm[:, 0:1], func=COPY)
+
+        nc.sync.dma_start(out=gate_sb[:], in_=gate.rearrange("(p i) -> p i", i=TILES))
+        nc.sync.dma_start(out=gain_row[0:1, :], in_=gain.rearrange("(o d) -> o d", o=1))
+        nc.sync.dma_start(out=ws_scale_sb[:], in_=ws_scale.rearrange("(g p t) o -> p g (t o)", p=P, t=4))
+        load_hr(0, 0)
+        load_ws(0)
+        load_planes(wr_planes, wr_scales)
+        load_wr(0)
+        load_hr(0, 1)
+        load_wr(2)
+        load_hr(1)
+        load_ws(1)
+        load_hs(0)
+        load_hs(1)
+        load_hr(2)
+        load_hs(2)
+        load_hr(3)
+        load_hs(3)
+        load_planes(wo_planes, wo_scales)
+        load_resid(0)
+        nc.sync.dma_start(out=wo_sb[:], in_=wo_words.rearrange("g p n -> p g n"))
+        load_resid(1)
+        load_hr(4)
+        load_hs(4)
+        load_resid(2)
+        for i in range(5, TILES):
+            load_hr(i)
+            load_hs(i)
+            load_resid(i - 2)
+        load_resid(6)
+        load_resid(7)
+
+        gain_banks = [bank_tile(6 + h, [P, BANK]) for h in range(HALVES)]
+        for h in range(HALVES):
+            nc.tensor.matmul(gain_banks[h][:], lhsT=ones[:], rhs=gain_row[:, h * BANK : (h + 1) * BANK], start=True, stop=True)
+            nc.scalar.copy(out=gain_sb[:, h * BANK : (h + 1) * BANK], in_=gain_banks[h][:])
+
+        def routed(i, g0, g1):
+            for g in range(g0, g1):
+                for h in range(HALVES):
+                    routed_pass(i, h, g)
+
+        def act(i, b, k):
+            turn(("act", i, b), k)
+            collect(("act", i, b))
+
+        for i in range(PLAIN):
+            order_hs(i)
+        def shared(i, g):
+            for h in range(HALVES):
+                shared_pass(i, h, g)
+
+        apply_gate(0, 0)
+        act(0, 0, 1)
+        widen(0, 0, "v")
+        quantize(("act", 0, 0))
+        widen(0, 3)
+        widen(0, 2)
+        widen(0, 1, "v")
+        for h in range(HALVES):
+            open_half(0, h, (0, 3)[h])
+        routed(0, 0, 2)
+        apply_gate(0, 1)
+        act(0, 1, 2)
+        interleave(0, 0)
+        quantize(("act", 0, 1))
+        apply_gate(1, 0)
+        act(1, 0, 6)
+        routed(0, 2, 4)
+        apply_gate(1, 1)
+        act(1, 1, 7)
+        quantize_ws(0, 0)
+        quantize(("act", 1, 0))
+        act(0, 2, 1)
+        act(1, 2, 2)
+        interleave(0, 1)
+        quantize(("act", 1, 1))
+        for t in (3, 2):
+            widen(1, t)
+        for h in range(HALVES):
+            open_half(1, h, 4 + h)
+        routed(1, 0, 4)
+        widen(1, 0, "v")
+        quantize_ws(0, 1)
+        widen(1, 1, "v")
+        quantize(("act", 0, 2))
+        apply_gate(2, 0)
+        act(2, 0, 1)
+        apply_gate(2, 1)
+        act(2, 1, 2)
+        quantize(("act", 1, 2))
+        shared(0, 0)
+        shared(1, 0)
+        interleave(1, 0)
+        act(2, 2, 1)
+        quantize(("act", 2, 0))
+        quantize(("act", 2, 1))
+        for h in range(HALVES):
+            open_half(2, h, 6 + h)
+        routed(2, 0, 4)
+        interleave(1, 1, "s")
+        quantize_ws(1, 0)
+        quantize(("act", 2, 2))
+        apply_gate(3, 0)
+        apply_gate(3, 1)
+        order_hs(3)
+        quantize_ws(1, 1)
+        shared(2, 0)
+        for b in range(3):
+            act(3, b, (2, 1, 2)[b])
+        apply_gate(4, 0)
+        apply_gate(4, 1)
+        for i in range(3):
+            shared(i, 1)
+        scale_pair(0, 0)
+        for b in range(3):
+            quantize(("act", 3, b))
+        scale_pair(0, 1)
+        order_hs(4)
+        add_resid(0, 0)
+        add_resid(0, 1)
+        scale_pair(1, 0)
+        scale_pair(1, 1)
+        scale_pair(2, 0)
+        live["bank"] = -1
+
+        def half(i, h):
+            open_half(i, h)
+            for g in range(R_PASSES):
+                routed_pass(i, h, g)
+            for g in range(S_PASSES):
+                shared_pass(i, h, g)
+
+        def turn_z(i):
+            turn(("z", i))
+            collect(("z", i))
+
+        def add_both(i):
+            for h in range(HALVES):
+                add_resid(i, h)
+
+        last = TILES - 1
+        for i in range(3, TILES):
+            half(i, 0)
+            scale_pair(i - 1, 1)
+            if i < last:
+                for b in range(3):
+                    turn(("act", i + 1, b))
+                    collect(("act", i + 1, b))
+            turn_z(i - LAG)
+            if i == last:
+                turn_z(i - 2)
+            scale_pair(i, 0)
+            if i < last:
+                for b in range(3):
+                    quantize(("act", i + 1, b))
+            quantize(("z", i - LAG))
+            half(i, 1)
+            if i + 2 < TILES:
+                order_hs(i + 2)
+            for n in range(OUT_BANKS):
+                project(i - LAG, n)
+                empty(i - LAG, n)
+            store(i - LAG)
+            if i + 2 < TILES:
+                apply_gate(i + 2, 0)
+                apply_gate(i + 2, 1)
+            if i < last:
+                add_both(i - 2)
+            if i >= last - 1:
+                add_both(i - 1)
+
+        scale_pair(last, 1)
+        quantize(("z", last - 2))
+        turn_z(last - 1)
+        add_both(last)
+        quantize(("z", last - 1))
+        for i in (last - 2, last - 1, last):
+            for n in range(OUT_BANKS):
+                project(i, n)
+                empty(i, n, "v" if n == 1 else None)
+                store(i, n)
+            if i == last - 2:
+                turn_z(last)
+                quantize(("z", last))

@@ -259,40 +259,33 @@ def tile_expert_pair_project_s3_kernel(
         nc.scalar.activation(out=warm[:, 1:2], in_=warm[:, 0:1], func=COPY)
 
         nc.sync.dma_start(out=gate_sb[:], in_=gate.rearrange("(p i) -> p i", i=TILES))
-        nc.sync.dma_start(out=gain_row[0:1, :], in_=gain.rearrange("(o d) -> o d", o=1))
         nc.sync.dma_start(out=ws_scale_sb[:], in_=ws_scale.rearrange("(g p t) o -> p g (t o)", p=P, t=4))
         load_hr(0, 0)
+        load_hr(0, 1)
+        load_hs(0)
         load_ws(0)
+        load_hr(1)
+        nc.sync.dma_start(out=gain_row[0:1, :], in_=gain.rearrange("(o d) -> o d", o=1))
+        load_ws(1)
         load_planes(wr_planes, wr_scales)
         load_wr(0)
-        load_hr(0, 1)
-        load_wr(2)
-        load_hr(1)
-        load_ws(1)
-        load_hs(0)
         load_hs(1)
         load_hr(2)
+        load_wr(2)
         load_hs(2)
         load_hr(3)
         load_hs(3)
-        load_planes(wo_planes, wo_scales)
         load_resid(0)
-        nc.sync.dma_start(out=wo_sb[:], in_=wo_words.rearrange("g p n -> p g n"))
-        load_resid(1)
         load_hr(4)
         load_hs(4)
-        load_resid(2)
+        load_planes(wo_planes, wo_scales)
+        nc.sync.dma_start(out=wo_sb[:], in_=wo_words.rearrange("g p n -> p g n"))
         for i in range(5, TILES):
+            load_resid(i - 4)
             load_hr(i)
             load_hs(i)
-            load_resid(i - 2)
-        load_resid(6)
-        load_resid(7)
-
-        gain_banks = [bank_tile(6 + h, [P, BANK]) for h in range(HALVES)]
-        for h in range(HALVES):
-            nc.tensor.matmul(gain_banks[h][:], lhsT=ones[:], rhs=gain_row[:, h * BANK : (h + 1) * BANK], start=True, stop=True)
-            nc.scalar.copy(out=gain_sb[:, h * BANK : (h + 1) * BANK], in_=gain_banks[h][:])
+        for i in range(4, TILES):
+            load_resid(i)
 
         def routed(i, g0, g1):
             for g in range(g0, g1):
@@ -305,81 +298,96 @@ def tile_expert_pair_project_s3_kernel(
 
         for i in range(PLAIN):
             order_hs(i)
-        def shared(i, g):
-            for h in range(HALVES):
-                shared_pass(i, h, g)
+        def shared(i):
+            for g in range(S_PASSES):
+                for h in range(HALVES):
+                    shared_pass(i, h, g)
 
-        apply_gate(0, 0)
-        act(0, 0, 1)
-        widen(0, 0, "v")
+        for b in range(2):
+            apply_gate(0, b)
+            turn(("act", 0, b), 1 + b)
+            collect(("act", 0, b))
+        turn(("act", 0, 2), 4)
+        gain_banks = [bank_tile(6 + h, [P, BANK]) for h in range(HALVES)]
+        for h in range(HALVES):
+            nc.tensor.matmul(gain_banks[h][:], lhsT=ones[:], rhs=gain_row[:, h * BANK : (h + 1) * BANK], start=True, stop=True)
+        widen(0, 1)
+        widen(0, 3, "v")
         quantize(("act", 0, 0))
-        widen(0, 3)
-        widen(0, 2)
-        widen(0, 1, "v")
+        widen(0, 2, "v")
+        for b in range(2):
+            apply_gate(1, b)
+            turn(("act", 1, b), 1 + b)
+        collect(("act", 0, 2))
+        widen(0, 0, "v")
+        quantize(("act", 0, 1))
+        collect(("act", 1, 0))
+        collect(("act", 1, 1))
+        for h in range(HALVES):
+            nc.scalar.copy(out=gain_sb[:, h * BANK : (h + 1) * BANK], in_=gain_banks[h][:])
+        widen(1, 3, "v")
+        interleave(0, 0)
+        interleave(0, 1, "s")
+        for b in range(2):
+            quantize(("act", 1, b))
         for h in range(HALVES):
             open_half(0, h, (0, 3)[h])
         routed(0, 0, 2)
-        apply_gate(0, 1)
-        act(0, 1, 2)
-        interleave(0, 0)
-        quantize(("act", 0, 1))
-        apply_gate(1, 0)
-        act(1, 0, 6)
-        routed(0, 2, 4)
-        apply_gate(1, 1)
-        act(1, 1, 7)
-        quantize_ws(0, 0)
-        quantize(("act", 1, 0))
-        act(0, 2, 1)
-        act(1, 2, 2)
-        interleave(0, 1)
-        quantize(("act", 1, 1))
-        for t in (3, 2):
-            widen(1, t)
         for h in range(HALVES):
             open_half(1, h, 4 + h)
-        routed(1, 0, 4)
-        widen(1, 0, "v")
-        quantize_ws(0, 1)
-        widen(1, 1, "v")
+        routed(1, 0, 2)
         quantize(("act", 0, 2))
-        apply_gate(2, 0)
-        act(2, 0, 1)
-        apply_gate(2, 1)
-        act(2, 1, 2)
+        for b in range(2):
+            apply_gate(2, b)
+            turn(("act", 2, b), 1 + b)
+        turn(("act", 1, 2), 7)
+        widen(1, 0, "v")
+        widen(1, 2, "v")
+        quantize_ws(0, 0)
+        widen(1, 1, "v")
+        quantize_ws(0, 1)
+        collect(("act", 1, 2))
+        collect(("act", 2, 0))
+        routed(0, 2, 4)
+        routed(1, 2, 4)
+        interleave(1, 1)
+        interleave(1, 0, "s")
         quantize(("act", 1, 2))
-        shared(0, 0)
-        shared(1, 0)
-        interleave(1, 0)
-        act(2, 2, 1)
+        apply_gate(3, 0)
+        collect(("act", 2, 1))
+        turn(("act", 2, 2), 6)
         quantize(("act", 2, 0))
+        quantize_ws(1, 1)
+        turn(("act", 3, 0), 1)
+        quantize_ws(1, 0)
+        apply_gate(3, 1)
+        shared(0)
+        order_hs(3, "v")
+        collect(("act", 3, 0))
+        collect(("act", 2, 2))
+        turn(("act", 3, 1), 2)
+        turn(("act", 3, 2), 1)
         quantize(("act", 2, 1))
+        scale_pair(0, 0)
+        apply_gate(4, 0)
+        shared(1)
+        collect(("act", 3, 1))
+        collect(("act", 3, 2))
+        order_hs(4)
+        quantize(("act", 2, 2))
         for h in range(HALVES):
             open_half(2, h, 6 + h)
         routed(2, 0, 4)
-        interleave(1, 1, "s")
-        quantize_ws(1, 0)
-        quantize(("act", 2, 2))
-        apply_gate(3, 0)
-        apply_gate(3, 1)
-        order_hs(3)
-        quantize_ws(1, 1)
-        shared(2, 0)
-        for b in range(3):
-            act(3, b, (2, 1, 2)[b])
-        apply_gate(4, 0)
-        apply_gate(4, 1)
-        for i in range(3):
-            shared(i, 1)
-        scale_pair(0, 0)
-        for b in range(3):
-            quantize(("act", 3, b))
         scale_pair(0, 1)
-        order_hs(4)
-        add_resid(0, 0)
-        add_resid(0, 1)
+        quantize(("act", 3, 0))
         scale_pair(1, 0)
+        quantize(("act", 3, 1))
+        shared(2)
+        apply_gate(4, 1)
+        quantize(("act", 3, 2))
+        add_resid(0, 0)
         scale_pair(1, 1)
+        add_resid(0, 1)
         scale_pair(2, 0)
         live["bank"] = -1
 

@@ -53,9 +53,7 @@ def tile_expert_pair_project_s3_kernel(
         wo_sb = keep.tile([P, HALVES, 2 * FEATURES], U8, name="wo_sb", align_bytes=256)
         wo_planes = keep.tile([P, HALVES, FEATURES // 4], I32, name="wo_planes", align_bytes=256)
         ident = keep.tile([P, P], F32, name="ident")
-        ones = keep.tile([P, P], BF16, name="ones")
-        gain_row = keep.tile([P, CHANNELS], BF16, name="gain_row")
-        gain_sb = keep.tile([P, CHANNELS], F32, name="gain_sb")
+        gain_sb = keep.tile([P, CHANNELS], BF16, name="gain_sb")
         hr_sb = [keep.tile([P, ROUTED], BF16, name="hr%d" % i) for i in range(TILES)]
         hs_sb = [keep.tile([P, SHARED], BF16, name="hs%d" % i) for i in range(TILES)]
         resid_sb = [keep.tile([P, CHANNELS], BF16, name="resid%d" % i) for i in range(TILES)]
@@ -79,8 +77,11 @@ def tile_expert_pair_project_s3_kernel(
         def load_wr(g):
             nc.sync.dma_start(out=wr_sb[:, g : g + 2, :], in_=wr_words[g : g + 2].rearrange("g p n -> p g n"))
 
-        def load_ws(g):
-            nc.sync.dma_start(out=ws_raw[g][:], in_=ws_bytes.rearrange("(g p t) n -> g p t n", p=P, t=4)[g])
+        def load_ws(g, t=None):
+            rows = slice(0, 4) if t is None else slice(t, t + 2)
+            nc.sync.dma_start(
+                out=ws_raw[g][:, rows, :], in_=ws_bytes.rearrange("(g p t) n -> g p t n", p=P, t=4)[g][:, rows, :]
+            )
 
         def load_planes(planes, scales):
             words = scales.bitcast(I32)
@@ -253,28 +254,27 @@ def tile_expert_pair_project_s3_kernel(
         nc.vector.memset(warm[:], 0.0)
         nc.vector.memset(wr_planes[:], 0)
         make_identity(nc, ident[:])
-        nc.gpsimd.memset(ones[:], 1.0)
-        nc.gpsimd.memset(gain_row[:].bitcast(I32), 0)
         nc.vector.memset(wo_planes[:], 0)
         nc.scalar.activation(out=warm[:, 1:2], in_=warm[:, 0:1], func=COPY)
 
         nc.sync.dma_start(out=gate_sb[:], in_=gate.rearrange("(p i) -> p i", i=TILES))
         nc.sync.dma_start(out=ws_scale_sb[:], in_=ws_scale.rearrange("(g p t) o -> p g (t o)", p=P, t=4))
         load_hr(0, 0)
+        load_ws(0, 0)
         load_hr(0, 1)
+        load_ws(0, 2)
         load_hs(0)
-        load_ws(0)
         load_hr(1)
-        nc.sync.dma_start(out=gain_row[0:1, :], in_=gain.rearrange("(o d) -> o d", o=1))
-        load_ws(1)
         load_planes(wr_planes, wr_scales)
         load_wr(0)
+        load_ws(1)
         load_hs(1)
         load_hr(2)
         load_wr(2)
         load_hs(2)
         load_hr(3)
         load_hs(3)
+        nc.sync.dma_start(out=gain_sb[:], in_=gain.partition_broadcast(128))
         load_resid(0)
         load_hr(4)
         load_hs(4)
@@ -303,30 +303,26 @@ def tile_expert_pair_project_s3_kernel(
                 for h in range(HALVES):
                     shared_pass(i, h, g)
 
-        for b in range(2):
-            apply_gate(0, b)
-            turn(("act", 0, b), 1 + b)
-            collect(("act", 0, b))
-        turn(("act", 0, 2), 4)
-        gain_banks = [bank_tile(6 + h, [P, BANK]) for h in range(HALVES)]
-        for h in range(HALVES):
-            nc.tensor.matmul(gain_banks[h][:], lhsT=ones[:], rhs=gain_row[:, h * BANK : (h + 1) * BANK], start=True, stop=True)
+        apply_gate(0, 0)
+        turn(("act", 0, 0), 1)
         widen(0, 1)
-        widen(0, 3, "v")
-        quantize(("act", 0, 0))
+        widen(0, 0, "v")
+        collect(("act", 0, 0))
+        apply_gate(0, 1)
+        turn(("act", 0, 1), 2)
         widen(0, 2, "v")
+        collect(("act", 0, 1))
+        turn(("act", 0, 2), 4)
+        quantize(("act", 0, 0))
+        widen(0, 3)
+        quantize(("act", 0, 1))
         for b in range(2):
             apply_gate(1, b)
-            turn(("act", 1, b), 1 + b)
+            turn(("act", 1, b), 6 + b)
         collect(("act", 0, 2))
-        widen(0, 0, "v")
-        quantize(("act", 0, 1))
+        interleave(0, 0)
         collect(("act", 1, 0))
         collect(("act", 1, 1))
-        for h in range(HALVES):
-            nc.scalar.copy(out=gain_sb[:, h * BANK : (h + 1) * BANK], in_=gain_banks[h][:])
-        widen(1, 3, "v")
-        interleave(0, 0)
         interleave(0, 1, "s")
         for b in range(2):
             quantize(("act", 1, b))
@@ -336,58 +332,57 @@ def tile_expert_pair_project_s3_kernel(
         for h in range(HALVES):
             open_half(1, h, 4 + h)
         routed(1, 0, 2)
-        quantize(("act", 0, 2))
+        widen(1, 3, "v")
+        widen(1, 0, "v")
         for b in range(2):
             apply_gate(2, b)
-            turn(("act", 2, b), 1 + b)
-        turn(("act", 1, 2), 7)
-        widen(1, 0, "v")
         widen(1, 2, "v")
-        quantize_ws(0, 0)
         widen(1, 1, "v")
-        quantize_ws(0, 1)
-        collect(("act", 1, 2))
-        collect(("act", 2, 0))
         routed(0, 2, 4)
+        for b in range(2):
+            turn(("act", 2, b), 1 + b)
         routed(1, 2, 4)
-        interleave(1, 1)
+        turn(("act", 1, 2), 6)
+        turn(("act", 2, 2), 7)
         interleave(1, 0, "s")
-        quantize(("act", 1, 2))
-        apply_gate(3, 0)
+        quantize_ws(0, 0)
+        quantize_ws(0, 1)
+        interleave(1, 1)
+        quantize(("act", 0, 2))
+        collect(("act", 2, 0))
         collect(("act", 2, 1))
-        turn(("act", 2, 2), 6)
-        quantize(("act", 2, 0))
-        quantize_ws(1, 1)
-        turn(("act", 3, 0), 1)
-        quantize_ws(1, 0)
-        apply_gate(3, 1)
-        shared(0)
-        order_hs(3, "v")
-        collect(("act", 3, 0))
+        collect(("act", 1, 2))
         collect(("act", 2, 2))
-        turn(("act", 3, 1), 2)
-        turn(("act", 3, 2), 1)
+        quantize_ws(1, 0)
+        quantize_ws(1, 1)
+        quantize(("act", 2, 0))
         quantize(("act", 2, 1))
-        scale_pair(0, 0)
-        apply_gate(4, 0)
-        shared(1)
-        collect(("act", 3, 1))
-        collect(("act", 3, 2))
-        order_hs(4)
-        quantize(("act", 2, 2))
+        shared(0)
         for h in range(HALVES):
             open_half(2, h, 6 + h)
         routed(2, 0, 4)
+        apply_gate(3, 0)
+        quantize(("act", 1, 2))
+        apply_gate(3, 1)
+        order_hs(3)
+        scale_pair(0, 0)
+        quantize(("act", 2, 2))
+        for b in range(3):
+            turn(("act", 3, b), (1, 2, 0)[b])
+            collect(("act", 3, b))
         scale_pair(0, 1)
-        quantize(("act", 3, 0))
-        scale_pair(1, 0)
-        quantize(("act", 3, 1))
-        shared(2)
-        apply_gate(4, 1)
-        quantize(("act", 3, 2))
+        apply_gate(4, 0)
+        shared(1)
         add_resid(0, 0)
-        scale_pair(1, 1)
+        quantize(("act", 3, 0))
         add_resid(0, 1)
+        shared(2)
+        order_hs(4)
+        quantize(("act", 3, 1))
+        quantize(("act", 3, 2))
+        scale_pair(1, 0)
+        apply_gate(4, 1)
+        scale_pair(1, 1)
         scale_pair(2, 0)
         live["bank"] = -1
 
@@ -410,18 +405,18 @@ def tile_expert_pair_project_s3_kernel(
         for i in range(3, TILES):
             half(i, 0)
             scale_pair(i - 1, 1)
+            turn_z(i - LAG)
             if i < last:
                 for b in range(3):
                     turn(("act", i + 1, b))
                     collect(("act", i + 1, b))
-            turn_z(i - LAG)
-            if i == last:
+            else:
                 turn_z(i - 2)
             scale_pair(i, 0)
+            quantize(("z", i - LAG))
             if i < last:
                 for b in range(3):
                     quantize(("act", i + 1, b))
-            quantize(("z", i - LAG))
             half(i, 1)
             if i + 2 < TILES:
                 order_hs(i + 2)

@@ -20,14 +20,19 @@ ADD = mybir.AluOpType.add
 COPY = mybir.ActivationFunctionType.Copy
 
 P = 128
-K_PASS = 512
+PACK = 4
+K_PASS = P * PACK
+UNIT = 2 * K_PASS
 BANK = 512
+BANKS = 8
 TILES = TOKENS // P
 R_PASSES = ROUTED // K_PASS
 S_PASSES = SHARED // K_PASS
+R_UNITS = ROUTED // UNIT
 HALVES = CHANNELS // BANK
 OUT_BANKS = FEATURES // BANK
-PLAIN = 3
+
+OPENING = 3
 LAG = 3
 
 
@@ -47,25 +52,36 @@ def tile_expert_pair_project_s3_kernel(
         out_rows = out.rearrange("(p i) n -> p i n", i=TILES)
 
         gate_sb = keep.tile([P, TILES], BF16, name="gate_sb")
-        ws_scale_sb = keep.tile([P, S_PASSES, 4], F32, name="ws_scale_sb")
-        wr_sb = keep.tile([P, R_PASSES, 2 * CHANNELS], U8, name="wr_sb", align_bytes=256)
-        wr_planes = keep.tile([P, R_PASSES, CHANNELS // 4], I32, name="wr_planes", align_bytes=256)
-        wo_sb = keep.tile([P, HALVES, 2 * FEATURES], U8, name="wo_sb", align_bytes=256)
-        wo_planes = keep.tile([P, HALVES, FEATURES // 4], I32, name="wo_planes", align_bytes=256)
-        ident = keep.tile([P, P], F32, name="ident")
         gain_sb = keep.tile([P, CHANNELS], BF16, name="gain_sb")
-        hr_sb = [keep.tile([P, ROUTED], BF16, name="hr%d" % i) for i in range(TILES)]
         hs_sb = [keep.tile([P, SHARED], BF16, name="hs%d" % i) for i in range(TILES)]
+        hr_sb = [keep.tile([P, ROUTED], BF16, name="hr%d" % i) for i in range(TILES)]
         resid_sb = [keep.tile([P, CHANNELS], BF16, name="resid%d" % i) for i in range(TILES)]
-        ws_raw = [keep.tile([P, 4, CHANNELS], U8, name="ws_raw%d" % g) for g in range(S_PASSES)]
-        ws_wide = [keep.tile([P, 4, CHANNELS], BF16, name="ws_wide%d" % g) for g in range(S_PASSES)]
-        ws_codes = [[keep.tile([P, BANK], U32, name="ws_codes%d%d" % (g, h), align_bytes=256) for h in range(HALVES)] for g in range(S_PASSES)]
-        ws_planes = [[keep.tile([P, BANK], U8, name="ws_planes%d%d" % (g, h), align_bytes=256) for h in range(HALVES)] for g in range(S_PASSES)]
+        wr_sb = keep.tile([P, R_PASSES, 2 * CHANNELS], U8, name="wr_sb", align_bytes=256)
+        wo_sb = keep.tile([P, HALVES, 2 * FEATURES], U8, name="wo_sb", align_bytes=256)
+        wr_planes = keep.tile([P, R_PASSES, CHANNELS // 4], I32, name="wr_planes", align_bytes=256)
+        wo_planes = keep.tile([P, HALVES, FEATURES // 4], I32, name="wo_planes", align_bytes=256)
+        ws_scale_sb = keep.tile([P, S_PASSES, PACK], F32, name="ws_scale_sb")
+        ws_raw = [keep.tile([P, PACK, CHANNELS], U8, name="ws_raw%d" % g) for g in range(S_PASSES)]
 
-        live = {}
+        ws_wide = [keep.tile([P, PACK, CHANNELS], BF16, name="ws_wide%d" % g) for g in range(S_PASSES)]
+        ws_parts = [(g, h) for g in range(S_PASSES) for h in range(HALVES)]
+        ws_codes = {gh: keep.tile([P, BANK], U32, name="ws_codes%d%d" % gh, align_bytes=256) for gh in ws_parts}
+        ws_planes = {gh: keep.tile([P, BANK], U8, name="ws_planes%d%d" % gh, align_bytes=256) for gh in ws_parts}
+        ws_packed = {}
 
-        def load_hr(i, b=None):
-            cols = slice(0, ROUTED) if b is None else slice(b * 1024, (b + 1) * 1024)
+        ident = keep.tile([P, P], F32, name="ident")
+        primer = keep.tile([P, 2], F32, name="primer")
+
+        units = {}
+        in_split_order = {}
+        turned = {}
+        grouped = {}
+        operands = {}
+        pair_banks = {}
+        scaled_pairs = {}
+        results = {}
+
+        def load_hr(i, cols=slice(0, ROUTED)):
             nc.sync.dma_start(out=hr_sb[i][:, cols], in_=hr_rows[:, i, cols])
 
         def load_hs(i):
@@ -74,116 +90,111 @@ def tile_expert_pair_project_s3_kernel(
         def load_resid(i):
             nc.sync.dma_start(out=resid_sb[i][:], in_=resid_rows[:, i, :])
 
+        def load_ws(g, rows=slice(0, PACK)):
+            by_pass = ws_bytes.rearrange("(g p t) n -> g p t n", p=P, t=PACK)
+            nc.sync.dma_start(out=ws_raw[g][:, rows, :], in_=by_pass[g][:, rows, :])
+
         def load_wr(g):
             nc.sync.dma_start(out=wr_sb[:, g : g + 2, :], in_=wr_words[g : g + 2].rearrange("g p n -> p g n"))
 
-        def load_ws(g, t=None):
-            rows = slice(0, 4) if t is None else slice(t, t + 2)
-            nc.sync.dma_start(
-                out=ws_raw[g][:, rows, :], in_=ws_bytes.rearrange("(g p t) n -> g p t n", p=P, t=4)[g][:, rows, :]
-            )
-
         def load_planes(planes, scales):
-            words = scales.bitcast(I32)
+            as_int = scales.bitcast(I32)
             for r in range(4):
-                nc.sync.dma_start(out=planes[r:P:32, :, :], in_=words[:, r:16:4, :].rearrange("g q n -> q g n"))
+                nc.sync.dma_start(out=planes[r:P:32, :, :], in_=as_int[:, r:16:4, :].rearrange("g q n -> q g n"))
+
+        def split(ap):
+            return ap.rearrange("p (w u e) -> p u w e", u=2, e=2)
 
         def apply_gate(i, b):
-            gated = work.tile([P, 1024], BF16, name="gated", bufs=6)
-            dst = gated[:]
-            src = hr_sb[i][:, b * 1024 : (b + 1) * 1024]
-            if i >= PLAIN:
-                dst = dst.rearrange("p (u w e) -> p u w e", u=2, e=2)
-                src = src.rearrange("p (w u e) -> p u w e", u=2, e=2)
-            nc.vector.tensor_scalar(out=dst, in0=src, scalar1=gate_sb[:, i : i + 1], scalar2=None, op0=MULT)
-            live["act", i, b] = gated
-
-        def order_hs(i, engine=None):
-            if i < PLAIN:
-                live["act", i, 2] = hs_sb[i]
-                return
-            ordered = work.tile([P, 1024], BF16, name="ordered", bufs=4)
-            dst = ordered[:].bitcast(F32).rearrange("p (u w) -> p u w", u=2)
-            src = hs_sb[i][:].bitcast(F32).rearrange("p (w u) -> p u w", u=2)
-            if engine == "v":
-                nc.vector.tensor_copy(out=dst, in_=src)
+            routed = work.tile([P, UNIT], BF16, name="routed", bufs=6)
+            source = hr_sb[i][:, b * UNIT : (b + 1) * UNIT]
+            in_split_order["act", i, b] = i >= OPENING
+            if i >= OPENING:
+                target, source = routed[:].rearrange("p (u w e) -> p u w e", u=2, e=2), split(source)
             else:
-                nc.scalar.copy(out=dst, in_=src)
-            live["act", i, 2] = ordered
+                target = routed[:]
+            nc.vector.tensor_scalar(out=target, in0=source, scalar1=gate_sb[:, i : i + 1], scalar2=None, op0=MULT)
+            units["act", i, b] = routed
+
+        def order_hs(i):
+            ordered = work.tile([P, UNIT], BF16, name="ordered", bufs=4)
+            nc.scalar.copy(
+                out=ordered[:].bitcast(F32).rearrange("p (u w) -> p u w", u=2),
+                in_=hs_sb[i][:].bitcast(F32).rearrange("p (w u) -> p u w", u=2),
+            )
+            in_split_order["act", i, 2] = True
+            units["act", i, 2] = ordered
 
         def bank_tile(k, shape):
             return psum.tile(shape, F32, name="bank%d" % k)
 
-        def next_bank():
-            live["bank"] = (live["bank"] + 1) % 8
-            return live["bank"]
-
-        def turn(key, k=None):
-            words = live[key][:].bitcast(F32)
-            bank = bank_tile(next_bank() if k is None else k, [P, 2, 2, P])
-            plain = key[0] == "act" and key[1] < PLAIN
+        def turn(key, k):
+            words = units[key][:].bitcast(F32)
+            bank = bank_tile(k, [P, 2, 2, P])
             for g in range(2):
                 for u in range(2):
-                    if plain:
-                        block = words[:, 2 * P * g + u : 2 * P * (g + 1) : 2]
-                    else:
+                    if in_split_order[key]:
                         block = words[:, (2 * u + g) * P : (2 * u + g + 1) * P]
+                    else:
+                        block = words[:, 2 * P * g + u : 2 * P * (g + 1) : 2]
                     nc.tensor.transpose(bank[:, g, u, :], block, ident[:])
-            live["T", key] = bank
+            turned[key] = bank
 
-        def collect(key, engine=None):
-            grouped = work.tile([P, 1024], BF16, name="grouped", bufs=6, align_bytes=256)
-            dst = grouped[:].bitcast(F32).rearrange("p (g r u) -> p g r u", g=2, u=2)
-            src = live["T", key][:].rearrange("p g u r -> p g r u")
-            if engine == "v":
-                nc.vector.tensor_copy(out=dst, in_=src)
-            else:
-                nc.scalar.copy(out=dst, in_=src)
-            live["G", key] = grouped
+        def collect(key, copy):
+            rows = work.tile([P, UNIT], BF16, name="grouped", bufs=6, align_bytes=256)
+            copy(
+                out=rows[:].bitcast(F32).rearrange("p (g r u) -> p g r u", g=2, u=2),
+                in_=turned[key][:].rearrange("p g u r -> p g r u"),
+            )
+            grouped[key] = rows
 
         def quantize(key):
             codes = work.tile([P, 2 * P], U32, name="codes", bufs=12, align_bytes=256)
             planes = work.tile([P, 2 * P], U8, name="planes", bufs=12, align_bytes=256)
-            nc.vector.quantize_mx(out=codes[:].bitcast(FP8X4), scales=planes[:], in_=live["G", key][:])
-            live["Q", key] = (codes, planes)
+            nc.vector.quantize_mx(out=codes[:].bitcast(FP8X4), scales=planes[:], in_=grouped[key][:])
+            operands[key] = (codes, planes)
 
-        def widen(g, t, engine=None):
-            dst = ws_wide[g][:, t, :]
-            src = ws_raw[g][:, t, :].bitcast(FP8)
-            scale = ws_scale_sb[:, g, t : t + 1]
-            if engine == "v":
-                nc.vector.tensor_scalar(out=dst, in0=src, scalar1=scale, scalar2=None, op0=MULT)
-            else:
-                nc.scalar.activation(out=dst, in_=src, func=COPY, scale=scale)
-
-        def interleave(g, h, engine=None):
-            packed = work.tile([P, BANK, 4], BF16, name="packed", bufs=4, align_bytes=256)
-            src = ws_wide[g][:, :, h * BANK : (h + 1) * BANK].rearrange("p t n -> p n t")
-            if engine == "s":
-                nc.scalar.copy(out=packed[:], in_=src)
-            else:
-                nc.vector.tensor_copy(out=packed[:], in_=src)
-            live["W", g, h] = packed
-
-        def quantize_ws(g, h):
-            nc.vector.quantize_mx(
-                out=ws_codes[g][h][:].bitcast(FP8X4),
-                scales=ws_planes[g][h][:],
-                in_=live["W", g, h][:].rearrange("p n t -> p (n t)"),
-            )
-
-        def open_half(i, h, k=None):
-            live["pair", i, h] = bank_tile(next_bank() if k is None else k, [P, BANK])
-
-        def lhs(key, g):
-            codes, planes = live["Q", key]
+        def stationary(key, g):
+            codes, planes = operands[key]
             cols = slice(g * P, (g + 1) * P)
             return codes[:, cols].bitcast(FP8X4), planes[:, cols]
 
+        def widen_on_vector(g, t):
+            nc.vector.tensor_scalar(
+                out=ws_wide[g][:, t, :],
+                in0=ws_raw[g][:, t, :].bitcast(FP8),
+                scalar1=ws_scale_sb[:, g, t : t + 1],
+                scalar2=None,
+                op0=MULT,
+            )
+
+        def widen_on_scalar(g, t):
+            nc.scalar.activation(
+                out=ws_wide[g][:, t, :],
+                in_=ws_raw[g][:, t, :].bitcast(FP8),
+                func=COPY,
+                scale=ws_scale_sb[:, g, t : t + 1],
+            )
+
+        def interleave(g, h, copy):
+            packed = work.tile([P, BANK, PACK], BF16, name="packed", bufs=4, align_bytes=256)
+            copy(out=packed[:], in_=ws_wide[g][:, :, h * BANK : (h + 1) * BANK].rearrange("p t n -> p n t"))
+            ws_packed[g, h] = packed
+
+        def quantize_ws(g, h):
+            nc.vector.quantize_mx(
+                out=ws_codes[g, h][:].bitcast(FP8X4),
+                scales=ws_planes[g, h][:],
+                in_=ws_packed[g, h][:].rearrange("p n t -> p (n t)"),
+            )
+
+        def open_pair(i, h, k):
+            pair_banks[i, h] = bank_tile(k, [P, BANK])
+
         def routed_pass(i, h, g):
-            codes, planes = lhs(("act", i, g // 2), g % 2)
+            codes, planes = stationary(("act", i, g // 2), g % 2)
             nc.tensor.matmul_mx(
-                out=live["pair", i, h][:],
+                out=pair_banks[i, h][:],
                 lhsT=codes,
                 lhsT_scale=planes,
                 rhs=wr_sb[:, g, 2 * h * BANK : 2 * (h + 1) * BANK].bitcast(FP4X4),
@@ -193,39 +204,55 @@ def tile_expert_pair_project_s3_kernel(
             )
 
         def shared_pass(i, h, g):
-            codes, planes = lhs(("act", i, 2), g)
+            codes, planes = stationary(("act", i, R_UNITS), g)
             nc.tensor.matmul_mx(
-                out=live["pair", i, h][:],
+                out=pair_banks[i, h][:],
                 lhsT=codes,
                 lhsT_scale=planes,
-                rhs=ws_codes[g][h][:].bitcast(FP8X4),
-                rhs_scale=ws_planes[g][h][:],
+                rhs=ws_codes[g, h][:].bitcast(FP8X4),
+                rhs_scale=ws_planes[g, h][:],
                 start=False,
                 stop=(g == S_PASSES - 1),
             )
 
+        def routed_unit(i, b):
+            for g in (2 * b, 2 * b + 1):
+                for h in range(HALVES):
+                    routed_pass(i, h, g)
+
+        def shared_unit(i):
+            for g in range(S_PASSES):
+                for h in range(HALVES):
+                    shared_pass(i, h, g)
+
+        def half_pair(i, h, k):
+            open_pair(i, h, k)
+            for g in range(R_PASSES):
+                routed_pass(i, h, g)
+            for g in range(S_PASSES):
+                shared_pass(i, h, g)
+
         def scale_pair(i, h):
             scaled = work.tile([P, BANK], F32, name="scaled", bufs=8)
-            nc.vector.tensor_tensor(
-                out=scaled[:], in0=live["pair", i, h][:], in1=gain_sb[:, h * BANK : (h + 1) * BANK], op=MULT
-            )
-            live["scaled", i, h] = scaled
+            channels = slice(h * BANK, (h + 1) * BANK)
+            nc.vector.tensor_tensor(out=scaled[:], in0=pair_banks[i, h][:], in1=gain_sb[:, channels], op=MULT)
+            scaled_pairs[i, h] = scaled
 
         def add_resid(i, h):
             if h == 0:
-                live["z", i] = work.tile([P, 1024], BF16, name="z", bufs=4)
-            order = "p (w u e) -> p u w e"
+                units["z", i] = work.tile([P, UNIT], BF16, name="z", bufs=4)
+                in_split_order["z", i] = True
             nc.vector.tensor_tensor(
-                out=live["z", i][:].rearrange("p (u g w e) -> p g u w e", u=2, g=2, e=2)[:, h],
-                in0=live["scaled", i, h][:].rearrange(order, u=2, e=2),
-                in1=resid_sb[i][:, h * BANK : (h + 1) * BANK].rearrange(order, u=2, e=2),
+                out=units["z", i][:].rearrange("p (u g w e) -> p g u w e", u=2, g=2, e=2)[:, h],
+                in0=split(scaled_pairs[i, h][:]),
+                in1=split(resid_sb[i][:, h * BANK : (h + 1) * BANK]),
                 op=ADD,
             )
 
-        def project(i, n):
-            bank = bank_tile(next_bank(), [P, BANK])
+        def project(i, n, k):
+            bank = bank_tile(k, [P, BANK])
             for g in range(HALVES):
-                codes, planes = lhs(("z", i), g)
+                codes, planes = stationary(("z", i), g)
                 nc.tensor.matmul_mx(
                     out=bank[:],
                     lhsT=codes,
@@ -235,46 +262,37 @@ def tile_expert_pair_project_s3_kernel(
                     start=(g == 0),
                     stop=(g == HALVES - 1),
                 )
-            live["out", i, n] = bank
-
-        def empty(i, n, engine=None):
             if n == 0:
-                live["res", i] = work.tile([P, FEATURES], F32, name="result", bufs=3)
-            dst = live["res", i][:, n * BANK : (n + 1) * BANK]
-            if engine == "v":
-                nc.vector.tensor_copy(out=dst, in_=live["out", i, n][:])
-            else:
-                nc.scalar.copy(out=dst, in_=live["out", i, n][:])
+                results[i] = work.tile([P, FEATURES], F32, name="result", bufs=3)
+            copy = nc.vector.tensor_copy if i >= TILES - LAG and n == 1 else nc.scalar.copy
+            copy(out=results[i][:, n * BANK : (n + 1) * BANK], in_=bank[:])
 
-        def store(i, n=None):
-            cols = slice(0, FEATURES) if n is None else slice(n * BANK, (n + 1) * BANK)
-            nc.sync.dma_start(out=out_rows[:, i, cols], in_=live["res", i][:, cols])
+        def store(i, cols=slice(0, FEATURES)):
+            nc.sync.dma_start(out=out_rows[:, i, cols], in_=results[i][:, cols])
 
-        warm = keep.tile([P, 2], F32, name="warm")
-        nc.vector.memset(warm[:], 0.0)
+        nc.vector.memset(primer[:], 0.0)
         nc.vector.memset(wr_planes[:], 0)
-        make_identity(nc, ident[:])
         nc.vector.memset(wo_planes[:], 0)
-        nc.scalar.activation(out=warm[:, 1:2], in_=warm[:, 0:1], func=COPY)
+        make_identity(nc, ident[:])
+        nc.scalar.activation(out=primer[:, 1:2], in_=primer[:, 0:1], func=COPY)
 
         nc.sync.dma_start(out=gate_sb[:], in_=gate.rearrange("(p i) -> p i", i=TILES))
-        nc.sync.dma_start(out=ws_scale_sb[:], in_=ws_scale.rearrange("(g p t) o -> p g (t o)", p=P, t=4))
-        load_hr(0, 0)
-        load_ws(0, 0)
-        load_hr(0, 1)
-        load_ws(0, 2)
+        nc.sync.dma_start(out=ws_scale_sb[:], in_=ws_scale.rearrange("(g p t) o -> p g (t o)", p=P, t=PACK))
+        for b in range(2):
+            load_hr(0, slice(b * UNIT, (b + 1) * UNIT))
+            load_ws(0, slice(2 * b, 2 * b + 2))
         load_hs(0)
         load_hr(1)
         load_planes(wr_planes, wr_scales)
         load_wr(0)
         load_ws(1)
-        load_hs(1)
-        load_hr(2)
         load_wr(2)
+        load_hr(2)
+        load_hs(1)
         load_hs(2)
         load_hr(3)
         load_hs(3)
-        nc.sync.dma_start(out=gain_sb[:], in_=gain.partition_broadcast(128))
+        nc.sync.dma_start(out=gain_sb[:], in_=gain.partition_broadcast(P))
         load_resid(0)
         load_hr(4)
         load_hs(4)
@@ -287,96 +305,83 @@ def tile_expert_pair_project_s3_kernel(
         for i in range(4, TILES):
             load_resid(i)
 
-        def routed(i, g0, g1):
-            for g in range(g0, g1):
-                for h in range(HALVES):
-                    routed_pass(i, h, g)
-
-        def act(i, b, k):
-            turn(("act", i, b), k)
-            collect(("act", i, b))
-
-        for i in range(PLAIN):
-            order_hs(i)
-        def shared(i):
-            for g in range(S_PASSES):
-                for h in range(HALVES):
-                    shared_pass(i, h, g)
+        on_vector, on_scalar = nc.vector.tensor_copy, nc.scalar.copy
+        for i in range(OPENING):
+            units["act", i, R_UNITS] = hs_sb[i]
+            in_split_order["act", i, R_UNITS] = False
+        pair_places = ((0, 3), (4, 5), (6, 7))
 
         apply_gate(0, 0)
         turn(("act", 0, 0), 1)
-        widen(0, 1)
-        widen(0, 0, "v")
-        collect(("act", 0, 0))
+        widen_on_scalar(0, 1)
+        widen_on_vector(0, 0)
+        collect(("act", 0, 0), on_scalar)
         apply_gate(0, 1)
         turn(("act", 0, 1), 2)
-        widen(0, 2, "v")
-        collect(("act", 0, 1))
+        widen_on_vector(0, 2)
+        collect(("act", 0, 1), on_scalar)
         turn(("act", 0, 2), 4)
         quantize(("act", 0, 0))
-        widen(0, 3)
-        quantize(("act", 0, 1))
-        for b in range(2):
+        widen_on_scalar(0, 3)
+        for b in range(R_UNITS):
             apply_gate(1, b)
             turn(("act", 1, b), 6 + b)
-        collect(("act", 0, 2))
-        interleave(0, 0)
-        collect(("act", 1, 0))
-        collect(("act", 1, 1))
-        interleave(0, 1, "s")
-        for b in range(2):
+        quantize(("act", 0, 1))
+        collect(("act", 0, 2), on_scalar)
+        interleave(0, 0, on_vector)
+        for b in range(R_UNITS):
+            collect(("act", 1, b), on_scalar)
+        interleave(0, 1, on_scalar)
+        for b in range(R_UNITS):
             quantize(("act", 1, b))
-        for h in range(HALVES):
-            open_half(0, h, (0, 3)[h])
-        routed(0, 0, 2)
-        for h in range(HALVES):
-            open_half(1, h, 4 + h)
-        routed(1, 0, 2)
-        widen(1, 3, "v")
-        widen(1, 0, "v")
-        for b in range(2):
+        for i in (0, 1):
+            for h in range(HALVES):
+                open_pair(i, h, pair_places[i][h])
+            routed_unit(i, 0)
+        for t in (3, 0, 2):
+            widen_on_vector(1, t)
+        for b in range(R_UNITS):
             apply_gate(2, b)
-        widen(1, 2, "v")
-        widen(1, 1, "v")
-        routed(0, 2, 4)
-        for b in range(2):
+        widen_on_scalar(1, 1)
+        routed_unit(0, 1)
+        for b in range(R_UNITS):
             turn(("act", 2, b), 1 + b)
-        routed(1, 2, 4)
+        routed_unit(1, 1)
         turn(("act", 1, 2), 6)
         turn(("act", 2, 2), 7)
-        interleave(1, 0, "s")
-        quantize_ws(0, 0)
-        quantize_ws(0, 1)
-        interleave(1, 1)
-        quantize(("act", 0, 2))
-        collect(("act", 2, 0))
-        collect(("act", 2, 1))
-        collect(("act", 1, 2))
-        collect(("act", 2, 2))
-        quantize_ws(1, 0)
-        quantize_ws(1, 1)
-        quantize(("act", 2, 0))
-        quantize(("act", 2, 1))
-        shared(0)
+        interleave(1, 0, on_scalar)
         for h in range(HALVES):
-            open_half(2, h, 6 + h)
-        routed(2, 0, 4)
+            quantize_ws(0, h)
+        interleave(1, 1, on_vector)
+        quantize(("act", 0, 2))
+        for b in range(3):
+            collect(("act", 2, b), on_scalar)
+        for h in (1, 0):
+            quantize_ws(1, h)
+        quantize(("act", 2, 0))
+        collect(("act", 1, 2), on_vector)
+        quantize(("act", 2, 1))
+        shared_unit(0)
+        for h in range(HALVES):
+            open_pair(2, h, pair_places[2][h])
+        for b in range(R_UNITS):
+            routed_unit(2, b)
         apply_gate(3, 0)
         quantize(("act", 1, 2))
         apply_gate(3, 1)
         order_hs(3)
         scale_pair(0, 0)
         quantize(("act", 2, 2))
-        for b in range(3):
-            turn(("act", 3, b), (1, 2, 0)[b])
-            collect(("act", 3, b))
+        for b, k in enumerate((1, 2, 0)):
+            turn(("act", 3, b), k)
+            collect(("act", 3, b), on_scalar)
         scale_pair(0, 1)
         apply_gate(4, 0)
-        shared(1)
+        shared_unit(1)
         add_resid(0, 0)
         quantize(("act", 3, 0))
         add_resid(0, 1)
-        shared(2)
+        shared_unit(2)
         order_hs(4)
         quantize(("act", 3, 1))
         quantize(("act", 3, 2))
@@ -384,64 +389,59 @@ def tile_expert_pair_project_s3_kernel(
         apply_gate(4, 1)
         scale_pair(1, 1)
         scale_pair(2, 0)
-        live["bank"] = -1
 
-        def half(i, h):
-            open_half(i, h)
-            for g in range(R_PASSES):
-                routed_pass(i, h, g)
-            for g in range(S_PASSES):
-                shared_pass(i, h, g)
+        taken = []
 
-        def turn_z(i):
-            turn(("z", i))
-            collect(("z", i))
+        def next_bank():
+            taken.append(len(taken) % BANKS)
+            return taken[-1]
 
-        def add_both(i):
-            for h in range(HALVES):
-                add_resid(i, h)
+        def turn_next(key):
+            turn(key, next_bank())
+            collect(key, on_scalar)
 
         last = TILES - 1
-        for i in range(3, TILES):
-            half(i, 0)
+        for i in range(OPENING, TILES):
+            half_pair(i, 0, next_bank())
             scale_pair(i - 1, 1)
-            turn_z(i - LAG)
+            turn_next(("z", i - LAG))
             if i < last:
                 for b in range(3):
-                    turn(("act", i + 1, b))
-                    collect(("act", i + 1, b))
+                    turn_next(("act", i + 1, b))
             else:
-                turn_z(i - 2)
+                turn_next(("z", i - LAG + 1))
             scale_pair(i, 0)
             quantize(("z", i - LAG))
             if i < last:
                 for b in range(3):
                     quantize(("act", i + 1, b))
-            half(i, 1)
+            half_pair(i, 1, next_bank())
             if i + 2 < TILES:
                 order_hs(i + 2)
             for n in range(OUT_BANKS):
-                project(i - LAG, n)
-                empty(i - LAG, n)
-            store(i - LAG)
-            if i + 2 < TILES:
-                apply_gate(i + 2, 0)
-                apply_gate(i + 2, 1)
+                project(i - LAG, n, next_bank())
+                if i == last:
+                    store(i - LAG, slice(n * BANK, (n + 1) * BANK))
             if i < last:
-                add_both(i - 2)
-            if i >= last - 1:
-                add_both(i - 1)
+                store(i - LAG)
+            if i + 2 < TILES:
+                for b in range(R_UNITS):
+                    apply_gate(i + 2, b)
+            ready = {last - 1: (i - 2, i - 1), last: (i - 1,)}.get(i, (i - 2,))
+            for j in ready:
+                for h in range(HALVES):
+                    add_resid(j, h)
 
         scale_pair(last, 1)
         quantize(("z", last - 2))
-        turn_z(last - 1)
-        add_both(last)
+        turn_next(("z", last - 1))
+        for h in range(HALVES):
+            add_resid(last, h)
         quantize(("z", last - 1))
-        for i in (last - 2, last - 1, last):
+        for i in range(last - 2, TILES):
             for n in range(OUT_BANKS):
-                project(i, n)
-                empty(i, n, "v" if n == 1 else None)
-                store(i, n)
+                project(i, n, next_bank())
+                store(i, slice(n * BANK, (n + 1) * BANK))
             if i == last - 2:
-                turn_z(last)
+                turn_next(("z", last))
                 quantize(("z", last))

from contextlib import ExitStack

import concourse.mybir as mybir
from concourse.masks import make_identity

TOKENS, SHARED, ROUTED, CHANNELS, FEATURES = 1024, 1024, 2048, 1024, 1536

FLOPS = 2 * TOKENS * CHANNELS * (SHARED + ROUTED) + 2 * TOKENS * CHANNELS * FEATURES

F32 = mybir.dt.float32
BF16 = mybir.dt.bfloat16
I32 = mybir.dt.int32
U32 = mybir.dt.uint32
U8 = mybir.dt.uint8
FP8 = mybir.dt.float8_e4m3fn
FP8X4 = mybir.dt.float8_e4m3fn_x4
FP4X4 = mybir.dt.float4_e2m1fn_x4
MULT = mybir.AluOpType.mult
ADD = mybir.AluOpType.add
COPY = mybir.ActivationFunctionType.Copy

P = 128
PACK = 4
K_PASS = P * PACK
UNIT = 2 * K_PASS
BANK = 512
BANKS = 8
TILES = TOKENS // P
R_PASSES = ROUTED // K_PASS
S_PASSES = SHARED // K_PASS
R_UNITS = ROUTED // UNIT
HALVES = CHANNELS // BANK
OUT_BANKS = FEATURES // BANK

OPENING = 3
LAG = 3


def tile_expert_pair_project_s3_kernel(
    tc, hs, hr, gate, ws_bytes, ws_scale, wr_words, wr_scales, gain, resid, wo_words, wo_scales, out
):
    nc = tc.nc
    with ExitStack() as ctx:
        keep = ctx.enter_context(tc.tile_pool(name="keep", bufs=1))
        work = ctx.enter_context(tc.tile_pool(name="work", bufs=3))
        psum = ctx.enter_context(tc.psum_pool(name="psum", bufs=1))
        ctx.enter_context(tc.manual_schedule())

        hs_rows = hs.rearrange("(p i) k -> p i k", i=TILES)
        hr_rows = hr.rearrange("(p i) k -> p i k", i=TILES)
        resid_rows = resid.rearrange("(p i) d -> p i d", i=TILES)
        out_rows = out.rearrange("(p i) n -> p i n", i=TILES)

        gate_sb = keep.tile([P, TILES], BF16, name="gate_sb")
        gain_sb = keep.tile([P, CHANNELS], BF16, name="gain_sb")
        hs_sb = [keep.tile([P, SHARED], BF16, name="hs%d" % i) for i in range(TILES)]
        hr_sb = [keep.tile([P, ROUTED], BF16, name="hr%d" % i) for i in range(TILES)]
        resid_sb = [keep.tile([P, CHANNELS], BF16, name="resid%d" % i) for i in range(TILES)]
        wr_sb = keep.tile([P, R_PASSES, 2 * CHANNELS], U8, name="wr_sb", align_bytes=256)
        wo_sb = keep.tile([P, HALVES, 2 * FEATURES], U8, name="wo_sb", align_bytes=256)
        wr_planes = keep.tile([P, R_PASSES, CHANNELS // 4], I32, name="wr_planes", align_bytes=256)
        wo_planes = keep.tile([P, HALVES, FEATURES // 4], I32, name="wo_planes", align_bytes=256)
        ws_scale_sb = keep.tile([P, S_PASSES, PACK], F32, name="ws_scale_sb")
        ws_raw = [keep.tile([P, PACK, CHANNELS], U8, name="ws_raw%d" % g) for g in range(S_PASSES)]

        ws_wide = [keep.tile([P, PACK, CHANNELS], BF16, name="ws_wide%d" % g) for g in range(S_PASSES)]
        ws_parts = [(g, h) for g in range(S_PASSES) for h in range(HALVES)]
        ws_codes = {gh: keep.tile([P, BANK], U32, name="ws_codes%d%d" % gh, align_bytes=256) for gh in ws_parts}
        ws_planes = {gh: keep.tile([P, BANK], U8, name="ws_planes%d%d" % gh, align_bytes=256) for gh in ws_parts}
        ws_packed = {}

        ident = keep.tile([P, P], F32, name="ident")
        primer = keep.tile([P, 2], F32, name="primer")

        units = {}
        in_split_order = {}
        turned = {}
        grouped = {}
        operands = {}
        pair_banks = {}
        scaled_pairs = {}
        results = {}

        def load_hr(i, cols=slice(0, ROUTED)):
            nc.sync.dma_start(out=hr_sb[i][:, cols], in_=hr_rows[:, i, cols])

        def load_hs(i):
            nc.sync.dma_start(out=hs_sb[i][:], in_=hs_rows[:, i, :])

        def load_resid(i):
            nc.sync.dma_start(out=resid_sb[i][:], in_=resid_rows[:, i, :])

        def load_ws(g, rows=slice(0, PACK)):
            by_pass = ws_bytes.rearrange("(g p t) n -> g p t n", p=P, t=PACK)
            nc.sync.dma_start(out=ws_raw[g][:, rows, :], in_=by_pass[g][:, rows, :])

        def load_wr(g):
            nc.sync.dma_start(out=wr_sb[:, g : g + 2, :], in_=wr_words[g : g + 2].rearrange("g p n -> p g n"))

        def load_planes(planes, scales):
            as_int = scales.bitcast(I32)
            for r in range(4):
                nc.sync.dma_start(out=planes[r:P:32, :, :], in_=as_int[:, r:16:4, :].rearrange("g q n -> q g n"))

        def split(ap):
            return ap.rearrange("p (w u e) -> p u w e", u=2, e=2)

        def apply_gate(i, b):
            routed = work.tile([P, UNIT], BF16, name="routed", bufs=6)
            source = hr_sb[i][:, b * UNIT : (b + 1) * UNIT]
            in_split_order["act", i, b] = i >= OPENING
            if i >= OPENING:
                target, source = routed[:].rearrange("p (u w e) -> p u w e", u=2, e=2), split(source)
            else:
                target = routed[:]
            nc.vector.tensor_scalar(out=target, in0=source, scalar1=gate_sb[:, i : i + 1], scalar2=None, op0=MULT)
            units["act", i, b] = routed

        def order_hs(i):
            ordered = work.tile([P, UNIT], BF16, name="ordered", bufs=4)
            nc.scalar.copy(
                out=ordered[:].bitcast(F32).rearrange("p (u w) -> p u w", u=2),
                in_=hs_sb[i][:].bitcast(F32).rearrange("p (w u) -> p u w", u=2),
            )
            in_split_order["act", i, 2] = True
            units["act", i, 2] = ordered

        def bank_tile(k, shape):
            return psum.tile(shape, F32, name="bank%d" % k)

        def turn(key, k):
            words = units[key][:].bitcast(F32)
            bank = bank_tile(k, [P, 2, 2, P])
            for g in range(2):
                for u in range(2):
                    if in_split_order[key]:
                        block = words[:, (2 * u + g) * P : (2 * u + g + 1) * P]
                    else:
                        block = words[:, 2 * P * g + u : 2 * P * (g + 1) : 2]
                    nc.tensor.transpose(bank[:, g, u, :], block, ident[:])
            turned[key] = bank

        def collect(key, copy):
            rows = work.tile([P, UNIT], BF16, name="grouped", bufs=6, align_bytes=256)
            copy(
                out=rows[:].bitcast(F32).rearrange("p (g r u) -> p g r u", g=2, u=2),
                in_=turned[key][:].rearrange("p g u r -> p g r u"),
            )
            grouped[key] = rows

        def quantize(key):
            codes = work.tile([P, 2 * P], U32, name="codes", bufs=12, align_bytes=256)
            planes = work.tile([P, 2 * P], U8, name="planes", bufs=12, align_bytes=256)
            nc.vector.quantize_mx(out=codes[:].bitcast(FP8X4), scales=planes[:], in_=grouped[key][:])
            operands[key] = (codes, planes)

        def stationary(key, g):
            codes, planes = operands[key]
            cols = slice(g * P, (g + 1) * P)
            return codes[:, cols].bitcast(FP8X4), planes[:, cols]

        def widen_on_vector(g, t):
            nc.vector.tensor_scalar(
                out=ws_wide[g][:, t, :],
                in0=ws_raw[g][:, t, :].bitcast(FP8),
                scalar1=ws_scale_sb[:, g, t : t + 1],
                scalar2=None,
                op0=MULT,
            )

        def widen_on_scalar(g, t):
            nc.scalar.activation(
                out=ws_wide[g][:, t, :],
                in_=ws_raw[g][:, t, :].bitcast(FP8),
                func=COPY,
                scale=ws_scale_sb[:, g, t : t + 1],
            )

        def interleave(g, h, copy):
            packed = work.tile([P, BANK, PACK], BF16, name="packed", bufs=4, align_bytes=256)
            copy(out=packed[:], in_=ws_wide[g][:, :, h * BANK : (h + 1) * BANK].rearrange("p t n -> p n t"))
            ws_packed[g, h] = packed

        def quantize_ws(g, h):
            nc.vector.quantize_mx(
                out=ws_codes[g, h][:].bitcast(FP8X4),
                scales=ws_planes[g, h][:],
                in_=ws_packed[g, h][:].rearrange("p n t -> p (n t)"),
            )

        def open_pair(i, h, k):
            pair_banks[i, h] = bank_tile(k, [P, BANK])

        def routed_pass(i, h, g):
            codes, planes = stationary(("act", i, g // 2), g % 2)
            nc.tensor.matmul_mx(
                out=pair_banks[i, h][:],
                lhsT=codes,
                lhsT_scale=planes,
                rhs=wr_sb[:, g, 2 * h * BANK : 2 * (h + 1) * BANK].bitcast(FP4X4),
                rhs_scale=wr_planes[:, g, h * BANK // 4 : (h + 1) * BANK // 4].bitcast(U8),
                start=(g == 0),
                stop=False,
            )

        def shared_pass(i, h, g):
            codes, planes = stationary(("act", i, R_UNITS), g)
            nc.tensor.matmul_mx(
                out=pair_banks[i, h][:],
                lhsT=codes,
                lhsT_scale=planes,
                rhs=ws_codes[g, h][:].bitcast(FP8X4),
                rhs_scale=ws_planes[g, h][:],
                start=False,
                stop=(g == S_PASSES - 1),
            )

        def routed_unit(i, b):
            for g in (2 * b, 2 * b + 1):
                for h in range(HALVES):
                    routed_pass(i, h, g)

        def shared_unit(i):
            for g in range(S_PASSES):
                for h in range(HALVES):
                    shared_pass(i, h, g)

        def half_pair(i, h, k):
            open_pair(i, h, k)
            for g in range(R_PASSES):
                routed_pass(i, h, g)
            for g in range(S_PASSES):
                shared_pass(i, h, g)

        def scale_pair(i, h):
            scaled = work.tile([P, BANK], F32, name="scaled", bufs=8)
            channels = slice(h * BANK, (h + 1) * BANK)
            nc.vector.tensor_tensor(out=scaled[:], in0=pair_banks[i, h][:], in1=gain_sb[:, channels], op=MULT)
            scaled_pairs[i, h] = scaled

        def add_resid(i, h):
            if h == 0:
                units["z", i] = work.tile([P, UNIT], BF16, name="z", bufs=4)
                in_split_order["z", i] = True
            nc.vector.tensor_tensor(
                out=units["z", i][:].rearrange("p (u g w e) -> p g u w e", u=2, g=2, e=2)[:, h],
                in0=split(scaled_pairs[i, h][:]),
                in1=split(resid_sb[i][:, h * BANK : (h + 1) * BANK]),
                op=ADD,
            )

        def project(i, n, k):
            bank = bank_tile(k, [P, BANK])
            for g in range(HALVES):
                codes, planes = stationary(("z", i), g)
                nc.tensor.matmul_mx(
                    out=bank[:],
                    lhsT=codes,
                    lhsT_scale=planes,
                    rhs=wo_sb[:, g, 2 * n * BANK : 2 * (n + 1) * BANK].bitcast(FP4X4),
                    rhs_scale=wo_planes[:, g, n * BANK // 4 : (n + 1) * BANK // 4].bitcast(U8),
                    start=(g == 0),
                    stop=(g == HALVES - 1),
                )
            if n == 0:
                results[i] = work.tile([P, FEATURES], F32, name="result", bufs=3)
            copy = nc.vector.tensor_copy if i >= TILES - LAG and n == 1 else nc.scalar.copy
            copy(out=results[i][:, n * BANK : (n + 1) * BANK], in_=bank[:])

        def store(i, cols=slice(0, FEATURES)):
            nc.sync.dma_start(out=out_rows[:, i, cols], in_=results[i][:, cols])

        nc.vector.memset(primer[:], 0.0)
        nc.vector.memset(wr_planes[:], 0)
        nc.vector.memset(wo_planes[:], 0)
        make_identity(nc, ident[:])
        nc.scalar.activation(out=primer[:, 1:2], in_=primer[:, 0:1], func=COPY)

        nc.sync.dma_start(out=gate_sb[:], in_=gate.rearrange("(p i) -> p i", i=TILES))
        nc.sync.dma_start(out=ws_scale_sb[:], in_=ws_scale.rearrange("(g p t) o -> p g (t o)", p=P, t=PACK))
        for b in range(2):
            load_hr(0, slice(b * UNIT, (b + 1) * UNIT))
            load_ws(0, slice(2 * b, 2 * b + 2))
        load_hs(0)
        load_hr(1)
        load_planes(wr_planes, wr_scales)
        load_wr(0)
        load_ws(1)
        load_wr(2)
        load_hr(2)
        load_hs(1)
        load_hs(2)
        load_hr(3)
        load_hs(3)
        nc.sync.dma_start(out=gain_sb[:], in_=gain.partition_broadcast(P))
        load_resid(0)
        load_hr(4)
        load_hs(4)
        load_planes(wo_planes, wo_scales)
        nc.sync.dma_start(out=wo_sb[:], in_=wo_words.rearrange("g p n -> p g n"))
        for i in range(5, TILES):
            load_resid(i - 4)
            load_hr(i)
            load_hs(i)
        for i in range(4, TILES):
            load_resid(i)

        on_vector, on_scalar = nc.vector.tensor_copy, nc.scalar.copy
        for i in range(OPENING):
            units["act", i, R_UNITS] = hs_sb[i]
            in_split_order["act", i, R_UNITS] = False
        pair_places = ((0, 3), (4, 5), (6, 7))

        apply_gate(0, 0)
        turn(("act", 0, 0), 1)
        widen_on_scalar(0, 1)
        widen_on_vector(0, 0)
        collect(("act", 0, 0), on_scalar)
        apply_gate(0, 1)
        turn(("act", 0, 1), 2)
        widen_on_vector(0, 2)
        collect(("act", 0, 1), on_scalar)
        turn(("act", 0, 2), 4)
        quantize(("act", 0, 0))
        widen_on_scalar(0, 3)
        for b in range(R_UNITS):
            apply_gate(1, b)
            turn(("act", 1, b), 6 + b)
        quantize(("act", 0, 1))
        collect(("act", 0, 2), on_scalar)
        interleave(0, 0, on_vector)
        for b in range(R_UNITS):
            collect(("act", 1, b), on_scalar)
        interleave(0, 1, on_scalar)
        for b in range(R_UNITS):
            quantize(("act", 1, b))
        for i in (0, 1):
            for h in range(HALVES):
                open_pair(i, h, pair_places[i][h])
            routed_unit(i, 0)
        for t in (3, 0, 2):
            widen_on_vector(1, t)
        for b in range(R_UNITS):
            apply_gate(2, b)
        widen_on_scalar(1, 1)
        routed_unit(0, 1)
        for b in range(R_UNITS):
            turn(("act", 2, b), 1 + b)
        routed_unit(1, 1)
        turn(("act", 1, 2), 6)
        turn(("act", 2, 2), 7)
        interleave(1, 0, on_scalar)
        for h in range(HALVES):
            quantize_ws(0, h)
        interleave(1, 1, on_vector)
        quantize(("act", 0, 2))
        for b in range(3):
            collect(("act", 2, b), on_scalar)
        for h in (1, 0):
            quantize_ws(1, h)
        quantize(("act", 2, 0))
        collect(("act", 1, 2), on_vector)
        quantize(("act", 2, 1))
        shared_unit(0)
        for h in range(HALVES):
            open_pair(2, h, pair_places[2][h])
        for b in range(R_UNITS):
            routed_unit(2, b)
        apply_gate(3, 0)
        quantize(("act", 1, 2))
        apply_gate(3, 1)
        order_hs(3)
        scale_pair(0, 0)
        quantize(("act", 2, 2))
        for b, k in enumerate((1, 2, 0)):
            turn(("act", 3, b), k)
            collect(("act", 3, b), on_scalar)
        scale_pair(0, 1)
        apply_gate(4, 0)
        shared_unit(1)
        add_resid(0, 0)
        quantize(("act", 3, 0))
        add_resid(0, 1)
        shared_unit(2)
        order_hs(4)
        quantize(("act", 3, 1))
        quantize(("act", 3, 2))
        scale_pair(1, 0)
        apply_gate(4, 1)
        scale_pair(1, 1)
        scale_pair(2, 0)

        taken = []

        def next_bank():
            taken.append(len(taken) % BANKS)
            return taken[-1]

        def turn_next(key):
            turn(key, next_bank())
            collect(key, on_scalar)

        last = TILES - 1
        for i in range(OPENING, TILES):
            half_pair(i, 0, next_bank())
            scale_pair(i - 1, 1)
            turn_next(("z", i - LAG))
            if i < last:
                for b in range(3):
                    turn_next(("act", i + 1, b))
            else:
                turn_next(("z", i - LAG + 1))
            scale_pair(i, 0)
            quantize(("z", i - LAG))
            if i < last:
                for b in range(3):
                    quantize(("act", i + 1, b))
            half_pair(i, 1, next_bank())
            if i + 2 < TILES:
                order_hs(i + 2)
            for n in range(OUT_BANKS):
                project(i - LAG, n, next_bank())
                if i == last:
                    store(i - LAG, slice(n * BANK, (n + 1) * BANK))
            if i < last:
                store(i - LAG)
            if i + 2 < TILES:
                for b in range(R_UNITS):
                    apply_gate(i + 2, b)
            ready = {last - 1: (i - 2, i - 1), last: (i - 1,)}.get(i, (i - 2,))
            for j in ready:
                for h in range(HALVES):
                    add_resid(j, h)

        scale_pair(last, 1)
        quantize(("z", last - 2))
        turn_next(("z", last - 1))
        for h in range(HALVES):
            add_resid(last, h)
        quantize(("z", last - 1))
        for i in range(last - 2, TILES):
            for n in range(OUT_BANKS):
                project(i, n, next_bank())
                store(i, slice(n * BANK, (n + 1) * BANK))
            if i == last - 2:
                turn_next(("z", last))
                quantize(("z", last))
